import numpy as np
import ml_dtypes


def mxq(x, axis, fmt="e4m3"):
    dtype, down = {"e4m3": (ml_dtypes.float8_e4m3fn, 7), "e5m2": (ml_dtypes.float8_e5m2, 14)}[fmt]
    v = np.moveaxis(np.asarray(x, np.float32).astype(ml_dtypes.bfloat16).astype(np.float64), axis, -1)
    blocks = v.reshape(v.shape[:-1] + (-1, 32))
    amax = np.abs(blocks).max(-1, keepdims=True)
    byte = np.maximum(np.where(amax > 0, np.frexp(amax)[1] - 1 + 127, 0) - down, 1)
    scale = np.exp2(byte - 127.0)
    codes = (blocks / scale).astype(np.float32).astype(dtype).astype(np.float64)
    return np.moveaxis((codes * scale).reshape(v.shape), -1, axis)


WIDE = False


def mx_kscale(k):
    if not WIDE:
        return np.ones(k)
    levels = np.array([10, -10, 5, -5, 0])
    if k % 512:
        return np.exp2(np.random.permutation(np.resize(levels, k // 32))).repeat(32)
    a = np.empty((k // 512, 16))
    for p in range(k // 512):
        a[p, :8] = np.random.permutation(np.resize(levels, 8))
        for g in range(8):
            far = levels[np.abs(levels - a[p, g]) >= 10]
            a[p, g + 8] = far[np.random.randint(len(far))]
    return np.exp2(a.ravel()).repeat(32)


def f64(x):
    return np.asarray(x).astype(np.float64)


def striped(idx):
    return np.tile(idx.reshape(-1, 16).T, (8, 1)).astype(np.uint16)


def unstriped(offs):
    return offs[:16].T.reshape(-1).astype(np.int64)


def striped8(idx):
    return np.concatenate([x.reshape(-1, 16).T for x in idx]).astype(np.uint16)


def runs(offs, k):
    lists = np.stack([offs[16 * r : 16 * r + 16].T.reshape(-1) for r in range(8)]).astype(np.int64)
    return lists[np.arange(k) % 512 // 64]


def pack_weight(w):
    k, n = w.shape
    w = f64(np.asarray(w, np.float32).astype(ml_dtypes.bfloat16)).reshape(k // 32, 32, n)
    amax = np.abs(w).max(1)
    byte = np.clip(np.where(amax > 0, np.frexp(amax)[1] - 1 + 127 - 7, 1), 1, 254)
    scaled = (w * np.exp2(127.0 - byte)[:, None, :]).reshape(k, n).astype(np.float32)
    words = np.ascontiguousarray(scaled.reshape(k // 512, 128, 4, n).transpose(0, 1, 3, 2)).astype(ml_dtypes.float8_e4m3fn).view(np.uint8)
    return words, np.ascontiguousarray(byte.astype(np.uint8).reshape(k // 512, 16, n))


def unpack_weight(words, scales):
    g, p, n, _ = words.shape
    vals = np.ascontiguousarray(words).view(ml_dtypes.float8_e4m3fn).astype(np.float64) * np.repeat(np.exp2(scales.astype(np.float64) - 127.0), 8, axis=1)[..., None]
    return vals.transpose(0, 1, 3, 2).reshape(g * 512, n)


def sigmoid(v):
    return 1.0 / (1.0 + np.exp(-np.maximum(v, -700.0)))


K, T, S, G, H, W = 512, 1024, 256, 2048, 512, 128


def setup_inputs():
    n = np.random.standard_normal
    s = mx_kscale(K)[:, None]
    packed_xT = pack_weight(n((K, T)) * s)
    packed_dT = pack_weight(n((K, G)) / s)
    perm = np.random.permutation(S)
    perm2 = np.random.permutation(S)
    perm3 = np.random.permutation(S)
    return {
        "x_words": packed_xT[0],
        "x_scales": packed_xT[1],
        "d_words": packed_dT[0],
        "d_scales": packed_dT[1],
        "sl": np.random.uniform(1.0, 2.0, (H, 1)).astype(np.float32),
        "th": (0.5 * n((H, 1))).astype(np.float32),
        "gs": (np.random.uniform(0.5, 1.5, (K, 1)) * s).astype(np.float32),
        "offs": striped(np.random.permutation(T)[:S]),
        "k1": striped8(np.random.randint(0, G, (8, H))),
        "hz": striped8(np.random.randint(0, T, (8, S))),
        "k2": striped8(np.random.randint(0, G, (8, H))),
        "hy": striped8(np.random.randint(0, T, (8, S))),
        "k3": striped8(np.random.randint(0, G, (8, H))),
        "n1": striped(perm[:W]),
        "n2": striped(perm[W:]),
        "n3": striped(perm2[:W]),
        "n4": striped(perm2[W:]),
        "n5": striped(np.random.permutation(S)),
        "k4": striped8(np.random.randint(0, G, (8, H))),
        "k5": striped8(np.random.randint(0, G, (8, H))),
        "two": striped(np.random.permutation(T)[:S]),
        "n6": striped(perm3[:W]),
        "n7": striped(perm3[W:]),
    }


def reference(x_words, x_scales, d_words, d_scales, sl, th, gs, offs, k1, hz, k2, hy, k3, n1, n2, n3, n4, n5, k4, k5, two, n6, n7):
    d_k4 = unpack_weight(d_words, d_scales)[np.arange(K)[:, None], runs(k4, K)]
    d_k1 = unpack_weight(d_words, d_scales)[np.arange(K)[:, None], runs(k1, K)]
    xq = unpack_weight(x_words, x_scales)[:, unstriped(offs)]
    d_k2 = unpack_weight(d_words, d_scales)[np.arange(K)[:, None], runs(k2, K)]
    x_hz = unpack_weight(x_words, x_scales)[np.arange(K)[:, None], runs(hz, K)]
    d_k3 = unpack_weight(d_words, d_scales)[np.arange(K)[:, None], runs(k3, K)]
    x_hy = unpack_weight(x_words, x_scales)[np.arange(K)[:, None], runs(hy, K)]
    h = 0.0625 * (d_k1.T @ xq + d_k2.T @ x_hz + d_k3.T @ x_hy)
    pa = h[:, unstriped(n1)]
    pb = h[:, unstriped(n2)]
    rb = np.minimum(pa, pb)
    ra = np.maximum(pa, pb)
    ua = np.zeros((H, S))
    ua[:, unstriped(n3)] = ra
    ub = ua.copy()
    ub[:, unstriped(n4)] = rb
    sg = sigmoid(f64(sl) * (ub[:, unstriped(n5)] - f64(th)))
    z = f64(gs) * (ub * sg)
    d_k5 = unpack_weight(d_words, d_scales)[np.arange(K)[:, None], runs(k5, K)]
    x_two = unpack_weight(x_words, x_scales)[:, unstriped(two)]
    h2 = 0.0625 * ((d_k4.T @ mxq(z, 0, "e4m3") + d_k5.T @ x_two))
    pa2 = h2[:, unstriped(n6)]
    pb2 = h2[:, unstriped(n7)]
    ra2 = np.maximum(pa2, pb2)
    out = h2.copy()
    out[:, unstriped(n6)] = ra2
    return out

@@ -1,0 +1,287 @@
+from contextlib import ExitStack
+
+import concourse.mybir as mybir
+from concourse.masks import make_identity
+
+K, T, S, G, H, W = 512, 1024, 256, 2048, 512, 128
+FLOPS = 5 * 2 * K * H * S
+
+F32 = mybir.dt.float32
+BF16 = mybir.dt.bfloat16
+U32 = mybir.dt.uint32
+I32 = mybir.dt.int32
+U16 = mybir.dt.uint16
+U8 = mybir.dt.uint8
+FP8X4 = mybir.dt.float8_e4m3fn_x4
+ACT = mybir.ActivationFunctionType
+ALU = mybir.AluOpType
+
+P = 128
+HALF = 256
+ALIGN = 64
+
+
+def tile_picked_mthhzmteordfill_none_p_kernel(
+    tc, x_words, x_scales, d_words, d_scales, sl, th, gs,
+    offs, k1, hz, k2, hy, k3, n1, n2, n3, n4, n5, k4, k5, two, n6, n7, out,
+):
+    nc = tc.nc
+    with ExitStack() as ctx:
+        keep = ctx.enter_context(tc.tile_pool(name="keep", bufs=1))
+        work = ctx.enter_context(tc.tile_pool(name="work", bufs=1))
+        acc_banks = ctx.enter_context(tc.psum_pool(name="acc", bufs=4))
+        turn_banks = ctx.enter_context(tc.psum_pool(name="turn", bufs=2))
+
+        def tile(shape, dtype, name, tag=None):
+            return work.tile(shape, dtype, name=name, tag=tag or name, align_bytes=ALIGN)
+
+        def load_list(ap, name):
+            t = keep.tile(list(ap.shape), U16, name=name)
+            nc.sync.dma_start(t[:], ap)
+            return t
+
+        def gather(dst, window, lst, first, count):
+            nc.vector.tensor_copy(dst, window[:].indirect(lst[:, first // 16 : (first + count) // 16]))
+
+        def place_scales(plane, picked):
+            for q in range(4):
+                nc.sync.dma_start(
+                    plane[32 * q : 32 * q + 4, :].bitcast(I32),
+                    picked[32 * q : 32 * q + 32 : 8, :].bitcast(I32),
+                )
+
+        xs = tile([P, T], U8, "xs")
+        ds = tile([P, G], U8, "ds")
+        xw = tile([P, T], U32, "xw")
+        dw = tile([P, G], U32, "dw")
+        plane1 = tile([P, 6 * HALF], U8, "plane1")
+        plane2 = tile([P, 3 * HALF], U8, "plane2")
+        plane3 = tile([P, S + H], U8, "plane3")
+        plane4 = tile([P, H], U8, "plane4")
+        zscale = [tile([P, P], U8, "zscale%d" % a) for a in range(2)]
+        nc.gpsimd.memset(xs[:].bitcast(I32), 0)
+        for t in (ds, plane1, plane2, plane3, plane4):
+            nc.vector.memset(t[:].bitcast(I32), 0)
+
+        nc.sync.dma_start(xs[0:P:8, :].bitcast(I32), x_scales[0].bitcast(I32))
+        l_offs, l_hz, l_hy = load_list(offs, "offs"), load_list(hz, "hz"), load_list(hy, "hy")
+        nc.sync.dma_start(ds[0:P:8, :].bitcast(I32), d_scales[0].bitcast(I32))
+        l_k1, l_k2, l_k3 = load_list(k1, "k1"), load_list(k2, "k2"), load_list(k3, "k3")
+        nc.sync.dma_start(xw[:].bitcast(I32), x_words[0].rearrange("p n t -> p (n t)").bitcast(I32))
+        nc.sync.dma_start(dw[:].bitcast(I32), d_words[0].rearrange("p n t -> p (n t)").bitcast(I32))
+        l_n1, l_n2 = load_list(n1, "n1"), load_list(n2, "n2")
+        l_n3, l_n4, l_n5 = load_list(n3, "n3"), load_list(n4, "n4"), load_list(n5, "n5")
+
+        x_lists, d_lists = (l_offs, l_hz, l_hy), (l_k1, l_k2, l_k3)
+
+        ident_bf = tile([P, P], BF16, "ident_bf")
+        ident_f32 = tile([P, P], F32, "ident_f32")
+        make_identity(nc, ident_bf[:])
+        make_identity(nc, ident_f32[:])
+
+        bytes1 = tile([P, 6 * HALF], U8, "bytes1", "bytes")
+        for a, lst in enumerate(x_lists):
+            gather(bytes1[:, a * HALF : (a + 1) * HALF], xs, lst, 0, S)
+        for a, lst in enumerate(d_lists):
+            gather(bytes1[:, (3 + a) * HALF : (4 + a) * HALF], ds, lst, 0, HALF)
+        place_scales(plane1, bytes1)
+
+        slope, level, gain = tile([P, 4], F32, "slope"), tile([P, 4], F32, "level"), tile([P, 4], F32, "gain")
+        with nc.allow_non_contiguous_dma(reason="one value a row"):
+            for t, vec in ((slope, sl), (level, th), (gain, gs)):
+                nc.sync.dma_start(t[:], vec.rearrange("(t p) o -> p (t o)", p=P))
+        l_two, l_k4, l_k5 = load_list(two, "two"), load_list(k4, "k4"), load_list(k5, "k5")
+        l_n6, l_n7 = load_list(n6, "n6"), load_list(n7, "n7")
+        slth = tile([P, 4], F32, "slth")
+        bias = tile([P, 4], F32, "bias")
+        nc.gpsimd.tensor_tensor(slth[:], slope[:], level[:], ALU.mult)
+        nc.gpsimd.tensor_scalar(bias[:], slth[:], -1.0, 0.0, ALU.mult, ALU.add)
+
+        xpick = tile([P, 3 * S], U32, "xpick")
+        for a, lst in enumerate(x_lists):
+            gather(xpick[:, a * S : (a + 1) * S], xw, lst, 0, S)
+        dpick1 = tile([P, 3 * HALF], U32, "dpick1")
+        for a, lst in enumerate(d_lists):
+            gather(dpick1[:, a * HALF : (a + 1) * HALF], dw, lst, 0, HALF)
+
+        def first_product(t, words, plane, base):
+            acc = acc_banks.tile([P, S], F32, name="acc")
+            for a in range(3):
+                c = a * HALF + (t % 2) * P
+                nc.tensor.matmul_mx(
+                    out=acc[:],
+                    lhsT=words[:, c : c + P].bitcast(FP8X4),
+                    lhsT_scale=plane[:, base + c : base + c + P],
+                    rhs=xpick[:, a * S : (a + 1) * S].bitcast(FP8X4),
+                    rhs_scale=plane1[:, a * S : (a + 1) * S],
+                    start=(a == 0),
+                    stop=(a == 2),
+                )
+            return acc
+
+        def leave_bank(acc, name, on_scalar):
+            h = tile([P, S], F32, name)
+            if on_scalar:
+                nc.scalar.activation(h[:], acc[:], ACT.Copy, scale=0.0625)
+            else:
+                nc.vector.tensor_scalar(h[:], acc[:], 0.0625, None, ALU.mult)
+            return h
+
+        def fetch_pairs(h, la, lb, name):
+            pair = tile([P, 2 * W], F32, name)
+            nc.scalar.activation(pair[:, :W], h[:].indirect(la[:]), ACT.Copy)
+            nc.scalar.activation(pair[:, W:], h[:].indirect(lb[:]), ACT.Copy)
+            return pair
+
+        def order_pairs(pair, t):
+            r = tile([P, 2 * W], F32, "r%d" % t)
+            nc.vector.tensor_tensor(r[:, :W], pair[:, :W], pair[:, W:], ALU.max)
+            nc.vector.tensor_tensor(r[:, W:], pair[:, :W], pair[:, W:], ALU.min)
+            return r
+
+        def put_and_gate(r, t):
+            ub = tile([P, S], F32, "ub%d" % t)
+            sg = tile([P, S], F32, "sg%d" % t)
+            nc.scalar.activation(ub[:].indirect(l_n3[:]), r[:, :W], ACT.Copy)
+            nc.scalar.activation(ub[:].indirect(l_n4[:]), r[:, W:], ACT.Copy)
+            for a in range(2):
+                nc.scalar.activation(
+                    sg[:, a * W : (a + 1) * W],
+                    ub[:].indirect(l_n5[:, a * W // 16 : (a + 1) * W // 16]),
+                    ACT.Sigmoid,
+                    scale=slope[:, t : t + 1],
+                    bias=bias[:, t : t + 1],
+                )
+            return ub, sg
+
+        zturn = tile([P, 2, 2, P], F32, "zturn")
+
+        def weigh(ub, sg, t, halves, tag=None):
+            zb = tile([P, len(halves) * W], BF16, "zb%d_%d" % (t, halves[0]), tag)
+            cols = slice(halves[0] * W, (halves[-1] + 1) * W)
+            nc.vector.scalar_tensor_tensor(zb[:], ub[:, cols], gain[:, t : t + 1], sg[:, cols], ALU.mult, ALU.mult)
+            return zb
+
+        def turn(zb, t, halves, engine_copy):
+            bank = turn_banks.tile([P, len(halves), P], BF16, name="bank1")
+            for a in range(len(halves)):
+                nc.tensor.transpose(bank[:, a, :], zb[:, a * W : (a + 1) * W], ident_bf[:])
+            engine_copy(
+                zturn[:, halves[0] : halves[-1] + 1, :, 32 * t : 32 * t + 32],
+                bank[:].bitcast(F32).rearrange("p a (m u) -> p a u m", u=2),
+            )
+
+        acc0 = first_product(0, dpick1, plane1, 3 * S)
+        acc1 = first_product(1, dpick1, plane1, 3 * S)
+
+        bytes2 = tile([P, 3 * HALF], U8, "bytes2", "bytes")
+        for a, lst in enumerate(d_lists):
+            gather(bytes2[:, a * HALF : (a + 1) * HALF], ds, lst, HALF, HALF)
+        place_scales(plane2, bytes2)
+
+        h0 = leave_bank(acc0, "h0", True)
+        pair0 = fetch_pairs(h0, l_n1, l_n2, "pair0")
+        h1 = leave_bank(acc1, "h1", True)
+        pair1 = fetch_pairs(h1, l_n1, l_n2, "pair1")
+        r0 = order_pairs(pair0, 0)
+        ub0, sg0 = put_and_gate(r0, 0)
+
+        dpick2 = tile([P, 3 * HALF], U32, "dpick2", "pair0")
+        for a, lst in enumerate(d_lists):
+            gather(dpick2[:, a * HALF : (a + 1) * HALF], dw, lst, HALF, HALF)
+        r1 = order_pairs(pair1, 1)
+        ub1, sg1 = put_and_gate(r1, 1)
+        two_words = tile([P, S], U32, "two_words", "pair1")
+        gather(two_words[:], xw, l_two, 0, S)
+
+        acc2 = first_product(2, dpick2, plane2, 0)
+        acc3 = first_product(3, dpick2, plane2, 0)
+        h2 = leave_bank(acc2, "h2", False)
+        h3 = leave_bank(acc3, "h3", False)
+        zb0 = weigh(ub0, sg0, 0, [0, 1], "pair0")
+        turn(zb0, 0, [0, 1], nc.vector.tensor_copy)
+
+        bytes3 = tile([P, S + H], U8, "bytes3", "sg0")
+        gather(bytes3[:, :S], xs, l_two, 0, S)
+        gather(bytes3[:, S:], ds, l_k4, 0, H)
+        place_scales(plane3, bytes3)
+
+        pair2 = fetch_pairs(h2, l_n1, l_n2, "pair2")
+        pair3 = fetch_pairs(h3, l_n1, l_n2, "pair3")
+        r2 = order_pairs(pair2, 2)
+        ub2, sg2 = put_and_gate(r2, 2)
+        zb1 = weigh(ub1, sg1, 1, [0, 1], "pair2")
+        turn(zb1, 1, [0, 1], nc.vector.tensor_copy)
+
+        bytes4 = tile([P, H], U8, "bytes4", "sg1")
+        gather(bytes4[:], ds, l_k5, 0, H)
+        place_scales(plane4, bytes4)
+
+        r3 = order_pairs(pair3, 3)
+        ub3, sg3 = put_and_gate(r3, 3)
+
+        dpick3 = tile([P, 2 * HALF], U32, "dpick3", "pair3")
+        for a, lst in enumerate((l_k4, l_k5)):
+            gather(dpick3[:, a * HALF : (a + 1) * HALF], dw, lst, 0, HALF)
+        zb2 = weigh(ub2, sg2, 2, [0, 1])
+        turn(zb2, 2, [0, 1], nc.vector.tensor_copy)
+
+        zb3 = [weigh(ub3, sg3, 3, [a]) for a in range(2)]
+        for a in range(2):
+            turn(zb3[a], 3, [a], nc.scalar.copy)
+        zwords = []
+        zrows = []
+        for a in range(2):
+            bank = turn_banks.tile([P, 2, P], F32, name="bank2")
+            for u in range(2):
+                nc.tensor.transpose(bank[:, u, :], zturn[:, a, u, :], ident_f32[:])
+            zr = tile([P, P, 2], F32, "zrows%d" % a)
+            copy = nc.vector.tensor_copy if a == 0 else nc.scalar.copy
+            copy(zr[:], bank[:].rearrange("p u j -> p j u"))
+            zrows.append(zr)
+        for a in range(2):
+            zw = tile([P, P], U32, "zwords%d" % a)
+            nc.vector.quantize_mx(
+                out=zw[:].bitcast(FP8X4),
+                scales=zscale[a][:],
+                in_=zrows[a][:].rearrange("p j u -> p (j u)").bitcast(BF16),
+            )
+            zwords.append(zw)
+
+        dpick4 = tile([P, 2 * HALF], U32, "dpick4", "zrows1")
+        for a, lst in enumerate((l_k4, l_k5)):
+            gather(dpick4[:, a * HALF : (a + 1) * HALF], dw, lst, HALF, HALF)
+
+        def second_product(m):
+            words = dpick3 if m < 2 else dpick4
+            c = (m % 2) * P
+            acc = acc_banks.tile([P, S], F32, name="acc")
+            nc.tensor.matmul_mx(
+                out=acc[:],
+                lhsT=words[:, HALF + c : HALF + c + P].bitcast(FP8X4),
+                lhsT_scale=plane4[:, m * P : (m + 1) * P],
+                rhs=two_words[:].bitcast(FP8X4),
+                rhs_scale=plane3[:, :S],
+                start=True,
+                stop=False,
+            )
+            for a in range(2):
+                nc.tensor.matmul_mx(
+                    out=acc[:, a * P : (a + 1) * P],
+                    lhsT=words[:, c : c + P].bitcast(FP8X4),
+                    lhsT_scale=plane3[:, S + m * P : S + (m + 1) * P],
+                    rhs=zwords[a][:].bitcast(FP8X4),
+                    rhs_scale=zscale[a][:],
+                    start=False,
+                    stop=(a == 1),
+                )
+            return acc
+
+        for m in range(4):
+            acc = second_product(m)
+            g = leave_bank(acc, "g%d" % m, m == 0)
+            pair = fetch_pairs(g, l_n6, l_n7, "last_pair%d" % m)
+            big = tile([P, W], F32, "big%d" % m)
+            nc.vector.tensor_tensor(big[:], pair[:, :W], pair[:, W:], ALU.max)
+            nc.scalar.activation(g[:].indirect(l_n6[:]), big[:], ACT.Copy)
+            nc.sync.dma_start(out[m * P : (m + 1) * P, :], g[:])

@@ -78,6 +78,8 @@ def tile_picked_mthhzmteordfill_none_p_kernel(
         ident_f32 = tile([P, P], F32, "ident_f32")
         make_identity(nc, ident_bf[:])
         make_identity(nc, ident_f32[:])
+        warm = tile([P, 1], F32, "warm")
+        nc.scalar.activation(warm[:], ident_f32[:, 0:1], ACT.Sigmoid)
 
         bytes1 = tile([P, 6 * HALF], U8, "bytes1", "bytes")
         for a, lst in enumerate(x_lists):

@@ -59,21 +59,25 @@ def tile_picked_mthhzmteordfill_none_p_kernel(
         plane3 = tile([P, S + H], U8, "plane3")
         plane4 = tile([P, H], U8, "plane4")
         zscale = [tile([P, P], U8, "zscale%d" % a) for a in range(2)]
-        nc.gpsimd.memset(xs[:].bitcast(I32), 0)
         for t in (ds, plane1, plane2, plane3, plane4):
             nc.vector.memset(t[:].bitcast(I32), 0)
 
-        nc.sync.dma_start(xs[0:P:8, :].bitcast(I32), x_scales[0].bitcast(I32))
+        nc.sync.dma_start(xs[:].bitcast(I32), x_scales[0].bitcast(I32).unsqueeze(1).to_broadcast([16, 8, T // 4]))
         l_offs, l_hz, l_hy = load_list(offs, "offs"), load_list(hz, "hz"), load_list(hy, "hy")
         nc.sync.dma_start(ds[0:P:8, :].bitcast(I32), d_scales[0].bitcast(I32))
         l_k1, l_k2, l_k3 = load_list(k1, "k1"), load_list(k2, "k2"), load_list(k3, "k3")
         nc.sync.dma_start(xw[:].bitcast(I32), x_words[0].rearrange("p n t -> p (n t)").bitcast(I32))
-        nc.sync.dma_start(dw[:].bitcast(I32), d_words[0].rearrange("p n t -> p (n t)").bitcast(I32))
         l_n1, l_n2 = load_list(n1, "n1"), load_list(n2, "n2")
         l_n3, l_n4, l_n5 = load_list(n3, "n3"), load_list(n4, "n4"), load_list(n5, "n5")
+        l_two = load_list(two, "two")
+        nc.sync.dma_start(dw[:].bitcast(I32), d_words[0].rearrange("p n t -> p (n t)").bitcast(I32))
 
         x_lists, d_lists = (l_offs, l_hz, l_hy), (l_k1, l_k2, l_k3)
 
+        vectors = tile([P, P], F32, "vectors")
+        nc.gpsimd.memset(vectors[:], 0.0)
+        for a, vec in enumerate((sl, th, gs)):
+            nc.gpsimd.dma_start(vectors[4 * a : 4 * a + 4, :], vec.rearrange("(t p) o -> t (p o)", p=P))
         ident_bf = tile([P, P], BF16, "ident_bf")
         ident_f32 = tile([P, P], F32, "ident_f32")
         make_identity(nc, ident_bf[:])
@@ -81,6 +85,11 @@ def tile_picked_mthhzmteordfill_none_p_kernel(
         warm = tile([P, 1], F32, "warm")
         nc.scalar.activation(warm[:], ident_f32[:, 0:1], ACT.Sigmoid)
 
+        bank = turn_banks.tile([P, P], F32, name="bank1")
+        nc.tensor.transpose(bank[:], vectors[:], ident_f32[:])
+        columns = tile([P, 12], F32, "columns")
+        nc.scalar.copy(columns[:], bank[:, :12])
+        slope, level, gain = columns[:, 0:4], columns[:, 4:8], columns[:, 8:12]
         bytes1 = tile([P, 6 * HALF], U8, "bytes1", "bytes")
         for a, lst in enumerate(x_lists):
             gather(bytes1[:, a * HALF : (a + 1) * HALF], xs, lst, 0, S)
@@ -88,15 +97,11 @@ def tile_picked_mthhzmteordfill_none_p_kernel(
             gather(bytes1[:, (3 + a) * HALF : (4 + a) * HALF], ds, lst, 0, HALF)
         place_scales(plane1, bytes1)
 
-        slope, level, gain = tile([P, 4], F32, "slope"), tile([P, 4], F32, "level"), tile([P, 4], F32, "gain")
-        with nc.allow_non_contiguous_dma(reason="one value a row"):
-            for t, vec in ((slope, sl), (level, th), (gain, gs)):
-                nc.sync.dma_start(t[:], vec.rearrange("(t p) o -> p (t o)", p=P))
-        l_two, l_k4, l_k5 = load_list(two, "two"), load_list(k4, "k4"), load_list(k5, "k5")
+        l_k4, l_k5 = load_list(k4, "k4"), load_list(k5, "k5")
         l_n6, l_n7 = load_list(n6, "n6"), load_list(n7, "n7")
         slth = tile([P, 4], F32, "slth")
         bias = tile([P, 4], F32, "bias")
-        nc.gpsimd.tensor_tensor(slth[:], slope[:], level[:], ALU.mult)
+        nc.gpsimd.tensor_tensor(slth[:], slope, level, ALU.mult)
         nc.gpsimd.tensor_scalar(bias[:], slth[:], -1.0, 0.0, ALU.mult, ALU.add)
 
         xpick = tile([P, 3 * S], U32, "xpick")
@@ -109,11 +114,11 @@ def tile_picked_mthhzmteordfill_none_p_kernel(
         def first_product(t, words, plane, base):
             acc = acc_banks.tile([P, S], F32, name="acc")
             for a in range(3):
-                c = a * HALF + (t % 2) * P
+                c = (t % 2) * P
                 nc.tensor.matmul_mx(
                     out=acc[:],
-                    lhsT=words[:, c : c + P].bitcast(FP8X4),
-                    lhsT_scale=plane[:, base + c : base + c + P],
+                    lhsT=words[a][:, c : c + P].bitcast(FP8X4),
+                    lhsT_scale=plane[:, base + a * HALF + c : base + a * HALF + c + P],
                     rhs=xpick[:, a * S : (a + 1) * S].bitcast(FP8X4),
                     rhs_scale=plane1[:, a * S : (a + 1) * S],
                     start=(a == 0),
@@ -135,129 +140,146 @@ def tile_picked_mthhzmteordfill_none_p_kernel(
             nc.scalar.activation(pair[:, W:], h[:].indirect(lb[:]), ACT.Copy)
             return pair
 
-        def order_pairs(pair, t):
-            r = tile([P, 2 * W], F32, "r%d" % t)
-            nc.vector.tensor_tensor(r[:, :W], pair[:, :W], pair[:, W:], ALU.max)
-            nc.vector.tensor_tensor(r[:, W:], pair[:, :W], pair[:, W:], ALU.min)
+        def pick(pair, op, name, tag=None):
+            r = tile([P, W], F32, name, tag)
+            nc.vector.tensor_tensor(r[:], pair[:, :W], pair[:, W:], op)
             return r
 
-        def put_and_gate(r, t):
-            ub = tile([P, S], F32, "ub%d" % t)
-            sg = tile([P, S], F32, "sg%d" % t)
-            nc.scalar.activation(ub[:].indirect(l_n3[:]), r[:, :W], ACT.Copy)
-            nc.scalar.activation(ub[:].indirect(l_n4[:]), r[:, W:], ACT.Copy)
-            for a in range(2):
-                nc.scalar.activation(
-                    sg[:, a * W : (a + 1) * W],
-                    ub[:].indirect(l_n5[:, a * W // 16 : (a + 1) * W // 16]),
-                    ACT.Sigmoid,
-                    scale=slope[:, t : t + 1],
-                    bias=bias[:, t : t + 1],
-                )
-            return ub, sg
+        def put(ub, lst, r):
+            nc.scalar.activation(ub[:].indirect(lst[:]), r[:], ACT.Copy)
 
-        zturn = tile([P, 2, 2, P], F32, "zturn")
-
-        def weigh(ub, sg, t, halves, tag=None):
-            zb = tile([P, len(halves) * W], BF16, "zb%d_%d" % (t, halves[0]), tag)
-            cols = slice(halves[0] * W, (halves[-1] + 1) * W)
-            nc.vector.scalar_tensor_tensor(zb[:], ub[:, cols], gain[:, t : t + 1], sg[:, cols], ALU.mult, ALU.mult)
-            return zb
-
-        def turn(zb, t, halves, engine_copy):
-            bank = turn_banks.tile([P, len(halves), P], BF16, name="bank1")
-            for a in range(len(halves)):
-                nc.tensor.transpose(bank[:, a, :], zb[:, a * W : (a + 1) * W], ident_bf[:])
-            engine_copy(
-                zturn[:, halves[0] : halves[-1] + 1, :, 32 * t : 32 * t + 32],
-                bank[:].bitcast(F32).rearrange("p a (m u) -> p a u m", u=2),
+        def gate(sg, ub, t, a):
+            nc.scalar.activation(
+                sg[:, a * W : (a + 1) * W],
+                ub[:].indirect(l_n5[:, a * W // 16 : (a + 1) * W // 16]),
+                ACT.Sigmoid,
+                scale=slope[:, t : t + 1],
+                bias=bias[:, t : t + 1],
             )
 
-        acc0 = first_product(0, dpick1, plane1, 3 * S)
-        acc1 = first_product(1, dpick1, plane1, 3 * S)
+        def weigh(t, cols, name, tag=None):
+            zb = tile([P, cols.stop - cols.start], BF16, name, tag)
+            nc.vector.scalar_tensor_tensor(zb[:], ub[t][:, cols], gain[:, t : t + 1], sg[t][:, cols], ALU.mult, ALU.mult)
+            return zb
 
-        bytes2 = tile([P, 3 * HALF], U8, "bytes2", "bytes")
-        for a, lst in enumerate(d_lists):
-            gather(bytes2[:, a * HALF : (a + 1) * HALF], ds, lst, HALF, HALF)
-        place_scales(plane2, bytes2)
+        ub = [tile([P, S], F32, "ub%d" % t) for t in range(4)]
+        sg = [tile([P, S], F32, "sg%d" % t) for t in range(4)]
+        zturn = tile([P, 2, 2, P], F32, "zturn")
+
+        dparts1 = [dpick1[:, a * HALF : (a + 1) * HALF] for a in range(3)]
+        acc0 = first_product(0, dparts1, plane1, 3 * S)
+        acc1 = first_product(1, dparts1, plane1, 3 * S)
+
+        bytes2a = tile([P, 2 * HALF], U8, "bytes2a", "bytes")
+        for a, lst in enumerate((l_k1, l_k2)):
+            gather(bytes2a[:, a * HALF : (a + 1) * HALF], ds, lst, HALF, HALF)
+        place_scales(plane2[:, : 2 * HALF], bytes2a)
 
         h0 = leave_bank(acc0, "h0", True)
         pair0 = fetch_pairs(h0, l_n1, l_n2, "pair0")
-        h1 = leave_bank(acc1, "h1", True)
+        h1 = leave_bank(acc1, "h1", False)
+        bytes2b = tile([P, HALF], U8, "bytes2b", "dpick1")
+        gather(bytes2b[:], ds, l_k3, HALF, HALF)
+        place_scales(plane2[:, 2 * HALF :], bytes2b)
         pair1 = fetch_pairs(h1, l_n1, l_n2, "pair1")
-        r0 = order_pairs(pair0, 0)
-        ub0, sg0 = put_and_gate(r0, 0)
+        big0 = pick(pair0, ALU.max, "big0")
+        dpick2a = tile([P, HALF], U32, "dpick2a", "h0")
+        gather(dpick2a[:], dw, l_k1, HALF, HALF)
+        big1 = pick(pair1, ALU.max, "big1")
+        small0 = pick(pair0, ALU.min, "small0", "h1")
+        small1 = pick(pair1, ALU.min, "small1")
+        put(ub[0], l_n3, big0)
+        put(ub[1], l_n3, big1)
+        put(ub[0], l_n4, small0)
+        put(ub[1], l_n4, small1)
+        for t in range(2):
+            for a in range(2):
+                gate(sg[t], ub[t], t, a)
 
-        dpick2 = tile([P, 3 * HALF], U32, "dpick2", "pair0")
-        for a, lst in enumerate(d_lists):
-            gather(dpick2[:, a * HALF : (a + 1) * HALF], dw, lst, HALF, HALF)
-        r1 = order_pairs(pair1, 1)
-        ub1, sg1 = put_and_gate(r1, 1)
+        dpick2b = tile([P, 2 * HALF], U32, "dpick2b", "pair0")
+        for a, lst in enumerate((l_k2, l_k3)):
+            gather(dpick2b[:, a * HALF : (a + 1) * HALF], dw, lst, HALF, HALF)
         two_words = tile([P, S], U32, "two_words", "pair1")
         gather(two_words[:], xw, l_two, 0, S)
 
-        acc2 = first_product(2, dpick2, plane2, 0)
-        acc3 = first_product(3, dpick2, plane2, 0)
+        dparts2 = [dpick2a[:], dpick2b[:, :HALF], dpick2b[:, HALF:]]
+        acc2 = first_product(2, dparts2, plane2, 0)
+        acc3 = first_product(3, dparts2, plane2, 0)
         h2 = leave_bank(acc2, "h2", False)
         h3 = leave_bank(acc3, "h3", False)
-        zb0 = weigh(ub0, sg0, 0, [0, 1], "pair0")
-        turn(zb0, 0, [0, 1], nc.vector.tensor_copy)
 
-        bytes3 = tile([P, S + H], U8, "bytes3", "sg0")
+        bytes3 = tile([P, S + H], U8, "bytes3", "xpick")
         gather(bytes3[:, :S], xs, l_two, 0, S)
         gather(bytes3[:, S:], ds, l_k4, 0, H)
         place_scales(plane3, bytes3)
+        zb0 = weigh(0, slice(0, S), "zb0", "pair0")
 
         pair2 = fetch_pairs(h2, l_n1, l_n2, "pair2")
         pair3 = fetch_pairs(h3, l_n1, l_n2, "pair3")
-        r2 = order_pairs(pair2, 2)
-        ub2, sg2 = put_and_gate(r2, 2)
-        zb1 = weigh(ub1, sg1, 1, [0, 1], "pair2")
-        turn(zb1, 1, [0, 1], nc.vector.tensor_copy)
+        big2 = pick(pair2, ALU.max, "big2")
+        zb1 = weigh(1, slice(0, S), "zb1", "h2")
+        big3 = pick(pair3, ALU.max, "big3")
+        small2 = pick(pair2, ALU.min, "small2", "h3")
+        small3 = pick(pair3, ALU.min, "small3")
+        put(ub[2], l_n3, big2)
+        put(ub[3], l_n3, big3)
+        put(ub[2], l_n4, small2)
+        put(ub[3], l_n4, small3)
+        for a in range(2):
+            for t in (2, 3):
+                gate(sg[t], ub[t], t, a)
 
-        bytes4 = tile([P, H], U8, "bytes4", "sg1")
+        bank = turn_banks.tile([P, 2, 2, P], BF16, name="bank1")
+        for t, zb in enumerate((zb0, zb1)):
+            for a in range(2):
+                nc.tensor.transpose(bank[:, a, t, :], zb[:, a * W : (a + 1) * W], ident_bf[:])
+        nc.vector.tensor_copy(
+            zturn[:, :, :, : P // 2],
+            bank[:].rearrange("p a t i -> p a (t i)").bitcast(F32).rearrange("p a (m u) -> p a u m", u=2),
+        )
+
+        bytes4 = tile([P, H], U8, "bytes4", "pair2")
         gather(bytes4[:], ds, l_k5, 0, H)
         place_scales(plane4, bytes4)
-
-        r3 = order_pairs(pair3, 3)
-        ub3, sg3 = put_and_gate(r3, 3)
-
         dpick3 = tile([P, 2 * HALF], U32, "dpick3", "pair3")
         for a, lst in enumerate((l_k4, l_k5)):
             gather(dpick3[:, a * HALF : (a + 1) * HALF], dw, lst, 0, HALF)
-        zb2 = weigh(ub2, sg2, 2, [0, 1])
-        turn(zb2, 2, [0, 1], nc.vector.tensor_copy)
 
-        zb3 = [weigh(ub3, sg3, 3, [a]) for a in range(2)]
         for a in range(2):
-            turn(zb3[a], 3, [a], nc.scalar.copy)
+            bank = turn_banks.tile([P, 2, P], BF16, name="bank1")
+            for t in (2, 3):
+                zb = weigh(t, slice(a * W, (a + 1) * W), "zb%d_%d" % (t, a))
+                nc.tensor.transpose(bank[:, t - 2, :], zb[:], ident_bf[:])
+            nc.scalar.copy(
+                zturn[:, a, :, P // 2 :],
+                bank[:].rearrange("p t i -> p (t i)").bitcast(F32).rearrange("p (m u) -> p u m", u=2),
+            )
+        dpick4 = tile([P, 2 * HALF], U32, "dpick4", "sg3")
+        for a, lst in enumerate((l_k4, l_k5)):
+            gather(dpick4[:, a * HALF : (a + 1) * HALF], dw, lst, HALF, HALF)
+
         zwords = []
-        zrows = []
         for a in range(2):
             bank = turn_banks.tile([P, 2, P], F32, name="bank2")
             for u in range(2):
                 nc.tensor.transpose(bank[:, u, :], zturn[:, a, u, :], ident_f32[:])
             zr = tile([P, P, 2], F32, "zrows%d" % a)
-            copy = nc.vector.tensor_copy if a == 0 else nc.scalar.copy
-            copy(zr[:], bank[:].rearrange("p u j -> p j u"))
-            zrows.append(zr)
-        for a in range(2):
+            nc.scalar.copy(zr[:], bank[:].rearrange("p u j -> p j u"))
             zw = tile([P, P], U32, "zwords%d" % a)
             nc.vector.quantize_mx(
                 out=zw[:].bitcast(FP8X4),
                 scales=zscale[a][:],
-                in_=zrows[a][:].rearrange("p j u -> p (j u)").bitcast(BF16),
+                in_=zr[:].rearrange("p j u -> p (j u)").bitcast(BF16),
             )
             zwords.append(zw)
-
-        dpick4 = tile([P, 2 * HALF], U32, "dpick4", "zrows1")
-        for a, lst in enumerate((l_k4, l_k5)):
-            gather(dpick4[:, a * HALF : (a + 1) * HALF], dw, lst, HALF, HALF)
 
         def second_product(m):
             words = dpick3 if m < 2 else dpick4
             c = (m % 2) * P
-            acc = acc_banks.tile([P, S], F32, name="acc")
+            if m < 2:
+                acc = acc_banks.tile([P, S], F32, name="acc")
+            else:
+                acc = turn_banks.tile([P, S], F32, name="bank2")
             nc.tensor.matmul_mx(
                 out=acc[:],
                 lhsT=words[:, HALF + c : HALF + c + P].bitcast(FP8X4),
@@ -283,7 +305,7 @@ def tile_picked_mthhzmteordfill_none_p_kernel(
             acc = second_product(m)
             g = leave_bank(acc, "g%d" % m, m == 0)
             pair = fetch_pairs(g, l_n6, l_n7, "last_pair%d" % m)
-            big = tile([P, W], F32, "big%d" % m)
+            big = tile([P, W], F32, "last_big%d" % m)
             nc.vector.tensor_tensor(big[:], pair[:, :W], pair[:, W:], ALU.max)
             nc.scalar.activation(g[:].indirect(l_n6[:]), big[:], ACT.Copy)
             nc.sync.dma_start(out[m * P : (m + 1) * P, :], g[:])

@@ -17,8 +17,14 @@ ACT = mybir.ActivationFunctionType
 ALU = mybir.AluOpType
 
 P = 128
-HALF = 256
+TILES = H // P
+HALF = H // 2
+GROUP = 16
+QUAD = 32
+BLOCK = 8
+SCALE_ROWS = K // 32
 ALIGN = 64
+SIXTEENTH = 0.0625
 
 
 def tile_picked_mthhzmteordfill_none_p_kernel(
@@ -27,285 +33,291 @@ def tile_picked_mthhzmteordfill_none_p_kernel(
 ):
     nc = tc.nc
     with ExitStack() as ctx:
-        keep = ctx.enter_context(tc.tile_pool(name="keep", bufs=1))
+        lists = ctx.enter_context(tc.tile_pool(name="lists", bufs=1))
         work = ctx.enter_context(tc.tile_pool(name="work", bufs=1))
-        acc_banks = ctx.enter_context(tc.psum_pool(name="acc", bufs=4))
-        turn_banks = ctx.enter_context(tc.psum_pool(name="turn", bufs=2))
+        sum_banks = ctx.enter_context(tc.psum_pool(name="sums", bufs=TILES))
+        turn_banks = ctx.enter_context(tc.psum_pool(name="turns", bufs=2))
 
-        def tile(shape, dtype, name, tag=None):
-            return work.tile(shape, dtype, name=name, tag=tag or name, align_bytes=ALIGN)
+        def tile(shape, dtype, name, over=None):
+            return work.tile(shape, dtype, name=name, tag=over or name, align_bytes=ALIGN)
 
         def load_list(ap, name):
-            t = keep.tile(list(ap.shape), U16, name=name)
-            nc.sync.dma_start(t[:], ap)
-            return t
+            offsets = lists.tile(list(ap.shape), U16, name=name)
+            nc.sync.dma_start(offsets[:], ap)
+            return offsets
 
-        def gather(dst, window, lst, first, count):
-            nc.vector.tensor_copy(dst, window[:].indirect(lst[:, first // 16 : (first + count) // 16]))
+        def entries(offsets, first, count):
+            return offsets[:, first // GROUP : (first + count) // GROUP]
+
+        def gather_parts(name, dtype, parts, over=None):
+            picked = tile([P, sum(part[3] for part in parts)], dtype, name, over)
+            at = 0
+            for window, offsets, first, count in parts:
+                nc.vector.tensor_copy(picked[:, at : at + count], window[:].indirect(entries(offsets, first, count)))
+                at = at + count
+            return picked
 
         def place_scales(plane, picked):
-            for q in range(4):
+            for q in range(P // QUAD):
                 nc.sync.dma_start(
-                    plane[32 * q : 32 * q + 4, :].bitcast(I32),
-                    picked[32 * q : 32 * q + 32 : 8, :].bitcast(I32),
+                    plane[QUAD * q : QUAD * q + QUAD // BLOCK, :].bitcast(I32),
+                    picked[QUAD * q : QUAD * (q + 1) : BLOCK, :].bitcast(I32),
                 )
 
-        xs = tile([P, T], U8, "xs")
-        ds = tile([P, G], U8, "ds")
-        xw = tile([P, T], U32, "xw")
-        dw = tile([P, G], U32, "dw")
-        plane1 = tile([P, 6 * HALF], U8, "plane1")
-        plane2 = tile([P, 3 * HALF], U8, "plane2")
-        plane3 = tile([P, S + H], U8, "plane3")
-        plane4 = tile([P, H], U8, "plane4")
-        zscale = [tile([P, P], U8, "zscale%d" % a) for a in range(2)]
-        for t in (ds, plane1, plane2, plane3, plane4):
-            nc.vector.memset(t[:].bitcast(I32), 0)
+        x_byte_table = tile([P, T], U8, "x_byte_table")
+        d_byte_table = tile([P, G], U8, "d_byte_table")
+        x_word_table = tile([P, T], U32, "x_word_table")
+        d_word_table = tile([P, G], U32, "d_word_table")
+        plane_first = tile([P, 3 * S + 3 * HALF], U8, "plane_first")
+        plane_second = tile([P, 3 * HALF], U8, "plane_second")
+        plane_two_k4 = tile([P, S + H], U8, "plane_two_k4")
+        plane_k5 = tile([P, H], U8, "plane_k5")
+        z_planes = [tile([P, W], U8, "z_plane%d" % a) for a in range(2)]
+        for zeroed in (d_byte_table, plane_first, plane_second, plane_two_k4, plane_k5):
+            nc.vector.memset(zeroed[:].bitcast(I32), 0)
 
-        nc.sync.dma_start(xs[:].bitcast(I32), x_scales[0].bitcast(I32).unsqueeze(1).to_broadcast([16, 8, T // 4]))
+        x_rows = x_scales[0].bitcast(I32).unsqueeze(1).to_broadcast([SCALE_ROWS, BLOCK, T // 4])
+        nc.scalar.dma_start(x_byte_table[:].bitcast(I32), x_rows)
         l_offs, l_hz, l_hy = load_list(offs, "offs"), load_list(hz, "hz"), load_list(hy, "hy")
-        nc.sync.dma_start(ds[0:P:8, :].bitcast(I32), d_scales[0].bitcast(I32))
+        nc.sync.dma_start(d_byte_table[0:P:BLOCK, :].bitcast(I32), d_scales[0].bitcast(I32))
         l_k1, l_k2, l_k3 = load_list(k1, "k1"), load_list(k2, "k2"), load_list(k3, "k3")
-        nc.sync.dma_start(xw[:].bitcast(I32), x_words[0].rearrange("p n t -> p (n t)").bitcast(I32))
+        nc.sync.dma_start(x_word_table[:].bitcast(I32), x_words[0].rearrange("p n t -> p (n t)").bitcast(I32))
         l_n1, l_n2 = load_list(n1, "n1"), load_list(n2, "n2")
         l_n3, l_n4, l_n5 = load_list(n3, "n3"), load_list(n4, "n4"), load_list(n5, "n5")
         l_two = load_list(two, "two")
-        nc.sync.dma_start(dw[:].bitcast(I32), d_words[0].rearrange("p n t -> p (n t)").bitcast(I32))
-
-        x_lists, d_lists = (l_offs, l_hz, l_hy), (l_k1, l_k2, l_k3)
+        nc.sync.dma_start(d_word_table[:].bitcast(I32), d_words[0].rearrange("p n t -> p (n t)").bitcast(I32))
 
         vectors = tile([P, P], F32, "vectors")
         nc.gpsimd.memset(vectors[:], 0.0)
-        for a, vec in enumerate((sl, th, gs)):
-            nc.gpsimd.dma_start(vectors[4 * a : 4 * a + 4, :], vec.rearrange("(t p) o -> t (p o)", p=P))
-        ident_bf = tile([P, P], BF16, "ident_bf")
+        for v, vec in enumerate((sl, th, gs)):
+            nc.gpsimd.dma_start(vectors[TILES * v : TILES * (v + 1), :], vec.rearrange("(t p) o -> t (p o)", p=P))
+        ident_bf16 = tile([P, P], BF16, "ident_bf16")
         ident_f32 = tile([P, P], F32, "ident_f32")
-        make_identity(nc, ident_bf[:])
+        make_identity(nc, ident_bf16[:])
         make_identity(nc, ident_f32[:])
         warm = tile([P, 1], F32, "warm")
         nc.scalar.activation(warm[:], ident_f32[:, 0:1], ACT.Sigmoid)
 
-        bank = turn_banks.tile([P, P], F32, name="bank1")
-        nc.tensor.transpose(bank[:], vectors[:], ident_f32[:])
-        columns = tile([P, 12], F32, "columns")
-        nc.scalar.copy(columns[:], bank[:, :12])
-        slope, level, gain = columns[:, 0:4], columns[:, 4:8], columns[:, 8:12]
-        bytes1 = tile([P, 6 * HALF], U8, "bytes1", "bytes")
-        for a, lst in enumerate(x_lists):
-            gather(bytes1[:, a * HALF : (a + 1) * HALF], xs, lst, 0, S)
-        for a, lst in enumerate(d_lists):
-            gather(bytes1[:, (3 + a) * HALF : (4 + a) * HALF], ds, lst, 0, HALF)
-        place_scales(plane1, bytes1)
+        vector_bank = turn_banks.tile([P, P], F32, name="turn_one")
+        nc.tensor.transpose(vector_bank[:], vectors[:], ident_f32[:])
+        columns = tile([P, 3 * TILES], F32, "columns")
+        nc.scalar.copy(columns[:], vector_bank[:, : 3 * TILES])
+        slope, level, gain = (columns[:, TILES * v : TILES * (v + 1)] for v in range(3))
+
+        x_lists, d_lists = (l_offs, l_hz, l_hy), (l_k1, l_k2, l_k3)
+        bytes_first = gather_parts(
+            "bytes_first", U8,
+            [(x_byte_table, lst, 0, S) for lst in x_lists] + [(d_byte_table, lst, 0, HALF) for lst in d_lists],
+        )
+        place_scales(plane_first, bytes_first)
 
         l_k4, l_k5 = load_list(k4, "k4"), load_list(k5, "k5")
         l_n6, l_n7 = load_list(n6, "n6"), load_list(n7, "n7")
-        slth = tile([P, 4], F32, "slth")
-        bias = tile([P, 4], F32, "bias")
-        nc.gpsimd.tensor_tensor(slth[:], slope, level, ALU.mult)
-        nc.gpsimd.tensor_scalar(bias[:], slth[:], -1.0, 0.0, ALU.mult, ALU.add)
+        slope_level = tile([P, TILES], F32, "slope_level")
+        bias = tile([P, TILES], F32, "bias")
+        nc.gpsimd.tensor_tensor(slope_level[:], slope, level, ALU.mult)
+        nc.gpsimd.tensor_scalar(bias[:], slope_level[:], -1.0, 0.0, ALU.mult, ALU.add)
 
-        xpick = tile([P, 3 * S], U32, "xpick")
-        for a, lst in enumerate(x_lists):
-            gather(xpick[:, a * S : (a + 1) * S], xw, lst, 0, S)
-        dpick1 = tile([P, 3 * HALF], U32, "dpick1")
-        for a, lst in enumerate(d_lists):
-            gather(dpick1[:, a * HALF : (a + 1) * HALF], dw, lst, 0, HALF)
+        x_picked = gather_parts("x_picked", U32, [(x_word_table, lst, 0, S) for lst in x_lists])
+        words_first = gather_parts("words_first", U32, [(d_word_table, lst, 0, HALF) for lst in d_lists])
 
-        def first_product(t, words, plane, base):
-            acc = acc_banks.tile([P, S], F32, name="acc")
-            for a in range(3):
-                c = (t % 2) * P
+        def sum_of_h(t, words, plane):
+            acc = sum_banks.tile([P, S], F32, name="acc")
+            c = (t % 2) * P
+            for n in range(3):
                 nc.tensor.matmul_mx(
                     out=acc[:],
-                    lhsT=words[a][:, c : c + P].bitcast(FP8X4),
-                    lhsT_scale=plane[:, base + a * HALF + c : base + a * HALF + c + P],
-                    rhs=xpick[:, a * S : (a + 1) * S].bitcast(FP8X4),
-                    rhs_scale=plane1[:, a * S : (a + 1) * S],
-                    start=(a == 0),
-                    stop=(a == 2),
+                    lhsT=words[n][:, c : c + P].bitcast(FP8X4),
+                    lhsT_scale=plane[:, n * HALF + c : n * HALF + c + P],
+                    rhs=x_picked[:, n * S : (n + 1) * S].bitcast(FP8X4),
+                    rhs_scale=plane_first[:, n * S : (n + 1) * S],
+                    start=(n == 0),
+                    stop=(n == 2),
                 )
             return acc
 
-        def leave_bank(acc, name, on_scalar):
-            h = tile([P, S], F32, name)
-            if on_scalar:
-                nc.scalar.activation(h[:], acc[:], ACT.Copy, scale=0.0625)
-            else:
-                nc.vector.tensor_scalar(h[:], acc[:], 0.0625, None, ALU.mult)
-            return h
+        def scale_on_scalar(dst, acc):
+            nc.scalar.activation(dst, acc[:], ACT.Copy, scale=SIXTEENTH)
 
-        def fetch_pairs(h, la, lb, name):
+        def scale_on_vector(dst, acc):
+            nc.vector.tensor_scalar(dst, acc[:], SIXTEENTH, None, ALU.mult)
+
+        def leave_bank(acc, name, scale_out):
+            result = tile([P, S], F32, name)
+            scale_out(result[:], acc)
+            return result
+
+        def fetch_pairs(rows, list_a, list_b, name):
             pair = tile([P, 2 * W], F32, name)
-            nc.scalar.activation(pair[:, :W], h[:].indirect(la[:]), ACT.Copy)
-            nc.scalar.activation(pair[:, W:], h[:].indirect(lb[:]), ACT.Copy)
+            nc.scalar.activation(pair[:, :W], rows[:].indirect(list_a[:]), ACT.Copy)
+            nc.scalar.activation(pair[:, W:], rows[:].indirect(list_b[:]), ACT.Copy)
             return pair
 
-        def pick(pair, op, name, tag=None):
-            r = tile([P, W], F32, name, tag)
-            nc.vector.tensor_tensor(r[:], pair[:, :W], pair[:, W:], op)
-            return r
+        def pick(pair, op, name, over=None):
+            chosen = tile([P, W], F32, name, over)
+            nc.vector.tensor_tensor(chosen[:], pair[:, :W], pair[:, W:], op)
+            return chosen
 
-        def put(ub, lst, r):
-            nc.scalar.activation(ub[:].indirect(lst[:]), r[:], ACT.Copy)
+        def put(window, offsets, values):
+            nc.scalar.activation(window[:].indirect(offsets[:]), values[:], ACT.Copy)
 
-        def gate(sg, ub, t, a):
+        ub = [tile([P, S], F32, "ub%d" % t) for t in range(TILES)]
+        sg = [tile([P, S], F32, "sg%d" % t) for t in range(TILES)]
+
+        def put_both(tiles, larger, smaller):
+            for offsets, values in ((l_n3, larger), (l_n4, smaller)):
+                for t, chosen in zip(tiles, values):
+                    put(ub[t], offsets, chosen)
+
+        def gate(t, a):
             nc.scalar.activation(
-                sg[:, a * W : (a + 1) * W],
-                ub[:].indirect(l_n5[:, a * W // 16 : (a + 1) * W // 16]),
+                sg[t][:, a * W : (a + 1) * W],
+                ub[t][:].indirect(entries(l_n5, a * W, W)),
                 ACT.Sigmoid,
                 scale=slope[:, t : t + 1],
                 bias=bias[:, t : t + 1],
             )
 
-        def weigh(t, cols, name, tag=None):
-            zb = tile([P, cols.stop - cols.start], BF16, name, tag)
-            nc.vector.scalar_tensor_tensor(zb[:], ub[t][:, cols], gain[:, t : t + 1], sg[t][:, cols], ALU.mult, ALU.mult)
-            return zb
+        def weigh(t, first, count, name, over=None):
+            z = tile([P, count], BF16, name, over)
+            cols = slice(first, first + count)
+            nc.vector.scalar_tensor_tensor(z[:], ub[t][:, cols], gain[:, t : t + 1], sg[t][:, cols], ALU.mult, ALU.mult)
+            return z
 
-        ub = [tile([P, S], F32, "ub%d" % t) for t in range(4)]
-        sg = [tile([P, S], F32, "sg%d" % t) for t in range(4)]
-        zturn = tile([P, 2, 2, P], F32, "zturn")
+        z_turned = tile([P, 2, 2, P], F32, "z_turned")
 
-        dparts1 = [dpick1[:, a * HALF : (a + 1) * HALF] for a in range(3)]
-        acc0 = first_product(0, dparts1, plane1, 3 * S)
-        acc1 = first_product(1, dparts1, plane1, 3 * S)
+        first_parts = [words_first[:, n * HALF : (n + 1) * HALF] for n in range(3)]
+        acc0 = sum_of_h(0, first_parts, plane_first[:, 3 * S :])
+        acc1 = sum_of_h(1, first_parts, plane_first[:, 3 * S :])
 
-        bytes2a = tile([P, 2 * HALF], U8, "bytes2a", "bytes")
-        for a, lst in enumerate((l_k1, l_k2)):
-            gather(bytes2a[:, a * HALF : (a + 1) * HALF], ds, lst, HALF, HALF)
-        place_scales(plane2[:, : 2 * HALF], bytes2a)
+        bytes_k12 = gather_parts(
+            "bytes_k12", U8, [(d_byte_table, lst, HALF, HALF) for lst in (l_k1, l_k2)], over="bytes_first"
+        )
+        place_scales(plane_second[:, : 2 * HALF], bytes_k12)
 
-        h0 = leave_bank(acc0, "h0", True)
+        h0 = leave_bank(acc0, "h0", scale_on_scalar)
         pair0 = fetch_pairs(h0, l_n1, l_n2, "pair0")
-        h1 = leave_bank(acc1, "h1", False)
-        bytes2b = tile([P, HALF], U8, "bytes2b", "dpick1")
-        gather(bytes2b[:], ds, l_k3, HALF, HALF)
-        place_scales(plane2[:, 2 * HALF :], bytes2b)
+        h1 = leave_bank(acc1, "h1", scale_on_vector)
+        bytes_k3 = gather_parts("bytes_k3", U8, [(d_byte_table, l_k3, HALF, HALF)], over="words_first")
+        place_scales(plane_second[:, 2 * HALF :], bytes_k3)
         pair1 = fetch_pairs(h1, l_n1, l_n2, "pair1")
-        big0 = pick(pair0, ALU.max, "big0")
-        dpick2a = tile([P, HALF], U32, "dpick2a", "h0")
-        gather(dpick2a[:], dw, l_k1, HALF, HALF)
-        big1 = pick(pair1, ALU.max, "big1")
-        small0 = pick(pair0, ALU.min, "small0", "h1")
-        small1 = pick(pair1, ALU.min, "small1")
-        put(ub[0], l_n3, big0)
-        put(ub[1], l_n3, big1)
-        put(ub[0], l_n4, small0)
-        put(ub[1], l_n4, small1)
-        for t in range(2):
+        larger0 = pick(pair0, ALU.max, "larger0")
+        words_k1 = gather_parts("words_k1", U32, [(d_word_table, l_k1, HALF, HALF)], over="h0")
+        larger1 = pick(pair1, ALU.max, "larger1")
+        smaller0 = pick(pair0, ALU.min, "smaller0", over="h1")
+        smaller1 = pick(pair1, ALU.min, "smaller1")
+        put_both((0, 1), (larger0, larger1), (smaller0, smaller1))
+        for t in (0, 1):
             for a in range(2):
-                gate(sg[t], ub[t], t, a)
+                gate(t, a)
 
-        dpick2b = tile([P, 2 * HALF], U32, "dpick2b", "pair0")
-        for a, lst in enumerate((l_k2, l_k3)):
-            gather(dpick2b[:, a * HALF : (a + 1) * HALF], dw, lst, HALF, HALF)
-        two_words = tile([P, S], U32, "two_words", "pair1")
-        gather(two_words[:], xw, l_two, 0, S)
+        words_k23 = gather_parts(
+            "words_k23", U32, [(d_word_table, lst, HALF, HALF) for lst in (l_k2, l_k3)], over="pair0"
+        )
+        words_two = gather_parts("words_two", U32, [(x_word_table, l_two, 0, S)], over="pair1")
 
-        dparts2 = [dpick2a[:], dpick2b[:, :HALF], dpick2b[:, HALF:]]
-        acc2 = first_product(2, dparts2, plane2, 0)
-        acc3 = first_product(3, dparts2, plane2, 0)
-        h2 = leave_bank(acc2, "h2", False)
-        h3 = leave_bank(acc3, "h3", False)
+        second_parts = [words_k1[:], words_k23[:, :HALF], words_k23[:, HALF:]]
+        acc2 = sum_of_h(2, second_parts, plane_second)
+        acc3 = sum_of_h(3, second_parts, plane_second)
+        h2 = leave_bank(acc2, "h2", scale_on_vector)
+        h3 = leave_bank(acc3, "h3", scale_on_vector)
 
-        bytes3 = tile([P, S + H], U8, "bytes3", "xpick")
-        gather(bytes3[:, :S], xs, l_two, 0, S)
-        gather(bytes3[:, S:], ds, l_k4, 0, H)
-        place_scales(plane3, bytes3)
-        zb0 = weigh(0, slice(0, S), "zb0", "pair0")
+        bytes_two_k4 = gather_parts(
+            "bytes_two_k4", U8, [(x_byte_table, l_two, 0, S), (d_byte_table, l_k4, 0, H)], over="x_picked"
+        )
+        place_scales(plane_two_k4, bytes_two_k4)
 
         pair2 = fetch_pairs(h2, l_n1, l_n2, "pair2")
         pair3 = fetch_pairs(h3, l_n1, l_n2, "pair3")
-        big2 = pick(pair2, ALU.max, "big2")
-        zb1 = weigh(1, slice(0, S), "zb1", "h2")
-        big3 = pick(pair3, ALU.max, "big3")
-        small2 = pick(pair2, ALU.min, "small2", "h3")
-        small3 = pick(pair3, ALU.min, "small3")
-        put(ub[2], l_n3, big2)
-        put(ub[3], l_n3, big3)
-        put(ub[2], l_n4, small2)
-        put(ub[3], l_n4, small3)
+        larger2 = pick(pair2, ALU.max, "larger2")
+        z0 = weigh(0, 0, S, "z0", over="h2")
+        larger3 = pick(pair3, ALU.max, "larger3")
+        smaller2 = pick(pair2, ALU.min, "smaller2", over="h3")
+        smaller3 = pick(pair3, ALU.min, "smaller3")
+        z1 = weigh(1, 0, S, "z1", over="pair2")
+        put_both((2, 3), (larger2, larger3), (smaller2, smaller3))
         for a in range(2):
             for t in (2, 3):
-                gate(sg[t], ub[t], t, a)
+                gate(t, a)
 
-        bank = turn_banks.tile([P, 2, 2, P], BF16, name="bank1")
-        for t, zb in enumerate((zb0, zb1)):
+        early_bank = turn_banks.tile([P, 2, 2, P], BF16, name="turn_one")
+        for t, z in enumerate((z0, z1)):
             for a in range(2):
-                nc.tensor.transpose(bank[:, a, t, :], zb[:, a * W : (a + 1) * W], ident_bf[:])
+                nc.tensor.transpose(early_bank[:, a, t, :], z[:, a * W : (a + 1) * W], ident_bf16[:])
         nc.vector.tensor_copy(
-            zturn[:, :, :, : P // 2],
-            bank[:].rearrange("p a t i -> p a (t i)").bitcast(F32).rearrange("p a (m u) -> p a u m", u=2),
+            z_turned[:, :, :, : P // 2],
+            early_bank[:].rearrange("j a t i -> j a (t i)").bitcast(F32).rearrange("j a (p u) -> j a u p", u=2),
         )
 
-        bytes4 = tile([P, H], U8, "bytes4", "pair2")
-        gather(bytes4[:], ds, l_k5, 0, H)
-        place_scales(plane4, bytes4)
-        dpick3 = tile([P, 2 * HALF], U32, "dpick3", "pair3")
-        for a, lst in enumerate((l_k4, l_k5)):
-            gather(dpick3[:, a * HALF : (a + 1) * HALF], dw, lst, 0, HALF)
+        bytes_k5 = gather_parts("bytes_k5", U8, [(d_byte_table, l_k5, 0, H)], over="pair3")
+        place_scales(plane_k5, bytes_k5)
+        words_low = gather_parts("words_low", U32, [(d_word_table, lst, 0, HALF) for lst in (l_k4, l_k5)], over="sg1")
 
         for a in range(2):
-            bank = turn_banks.tile([P, 2, P], BF16, name="bank1")
+            late_bank = turn_banks.tile([P, 2, P], BF16, name="turn_one")
             for t in (2, 3):
-                zb = weigh(t, slice(a * W, (a + 1) * W), "zb%d_%d" % (t, a))
-                nc.tensor.transpose(bank[:, t - 2, :], zb[:], ident_bf[:])
+                z = weigh(t, a * W, W, "z%d_%d" % (t, a))
+                nc.tensor.transpose(late_bank[:, t - 2, :], z[:], ident_bf16[:])
             nc.scalar.copy(
-                zturn[:, a, :, P // 2 :],
-                bank[:].rearrange("p t i -> p (t i)").bitcast(F32).rearrange("p (m u) -> p u m", u=2),
+                z_turned[:, a, :, P // 2 :],
+                late_bank[:].rearrange("j t i -> j (t i)").bitcast(F32).rearrange("j (p u) -> j u p", u=2),
             )
-        dpick4 = tile([P, 2 * HALF], U32, "dpick4", "sg3")
-        for a, lst in enumerate((l_k4, l_k5)):
-            gather(dpick4[:, a * HALF : (a + 1) * HALF], dw, lst, HALF, HALF)
+        words_high = gather_parts(
+            "words_high", U32, [(d_word_table, lst, HALF, HALF) for lst in (l_k4, l_k5)], over="sg3"
+        )
 
-        zwords = []
+        z_words = []
         for a in range(2):
-            bank = turn_banks.tile([P, 2, P], F32, name="bank2")
+            back_bank = turn_banks.tile([P, 2, P], F32, name="turn_two")
             for u in range(2):
-                nc.tensor.transpose(bank[:, u, :], zturn[:, a, u, :], ident_f32[:])
-            zr = tile([P, P, 2], F32, "zrows%d" % a)
-            nc.scalar.copy(zr[:], bank[:].rearrange("p u j -> p j u"))
-            zw = tile([P, P], U32, "zwords%d" % a)
+                nc.tensor.transpose(back_bank[:, u, :], z_turned[:, a, u, :], ident_f32[:])
+            z_rows = tile([P, W, 2], F32, "z_rows%d" % a)
+            nc.scalar.copy(z_rows[:], back_bank[:].rearrange("p u j -> p j u"))
+            codes = tile([P, W], U32, "z_words%d" % a)
             nc.vector.quantize_mx(
-                out=zw[:].bitcast(FP8X4),
-                scales=zscale[a][:],
-                in_=zr[:].rearrange("p j u -> p (j u)").bitcast(BF16),
+                out=codes[:].bitcast(FP8X4),
+                scales=z_planes[a][:],
+                in_=z_rows[:].rearrange("p j u -> p (j u)").bitcast(BF16),
             )
-            zwords.append(zw)
+            z_words.append(codes)
 
-        def second_product(m):
-            words = dpick3 if m < 2 else dpick4
+        def sum_of_h2(m, halves):
+            words = words_low if m < 2 else words_high
             c = (m % 2) * P
+            cols = slice(halves[0] * W, (halves[-1] + 1) * W)
             if m < 2:
-                acc = acc_banks.tile([P, S], F32, name="acc")
+                acc = sum_banks.tile([P, len(halves) * W], F32, name="acc")
             else:
-                acc = turn_banks.tile([P, S], F32, name="bank2")
+                acc = turn_banks.tile([P, len(halves) * W], F32, name="turn_two")
             nc.tensor.matmul_mx(
                 out=acc[:],
                 lhsT=words[:, HALF + c : HALF + c + P].bitcast(FP8X4),
-                lhsT_scale=plane4[:, m * P : (m + 1) * P],
-                rhs=two_words[:].bitcast(FP8X4),
-                rhs_scale=plane3[:, :S],
+                lhsT_scale=plane_k5[:, m * P : (m + 1) * P],
+                rhs=words_two[:, cols].bitcast(FP8X4),
+                rhs_scale=plane_two_k4[:, cols],
                 start=True,
                 stop=False,
             )
-            for a in range(2):
+            for a in halves:
                 nc.tensor.matmul_mx(
-                    out=acc[:, a * P : (a + 1) * P],
+                    out=acc[:, (a - halves[0]) * W : (a - halves[0] + 1) * W],
                     lhsT=words[:, c : c + P].bitcast(FP8X4),
-                    lhsT_scale=plane3[:, S + m * P : S + (m + 1) * P],
-                    rhs=zwords[a][:].bitcast(FP8X4),
-                    rhs_scale=zscale[a][:],
+                    lhsT_scale=plane_two_k4[:, S + m * P : S + (m + 1) * P],
+                    rhs=z_words[a][:].bitcast(FP8X4),
+                    rhs_scale=z_planes[a][:],
                     start=False,
-                    stop=(a == 1),
+                    stop=(a == halves[-1]),
                 )
             return acc
 
-        for m in range(4):
-            acc = second_product(m)
-            g = leave_bank(acc, "g%d" % m, m == 0)
-            pair = fetch_pairs(g, l_n6, l_n7, "last_pair%d" % m)
-            big = tile([P, W], F32, "last_big%d" % m)
-            nc.vector.tensor_tensor(big[:], pair[:, :W], pair[:, W:], ALU.max)
-            nc.scalar.activation(g[:].indirect(l_n6[:]), big[:], ACT.Copy)
-            nc.sync.dma_start(out[m * P : (m + 1) * P, :], g[:])
+        for m in range(TILES):
+            if m == 0:
+                result = tile([P, S], F32, "result0")
+                for a in range(2):
+                    scale_on_scalar(result[:, a * W : (a + 1) * W], sum_of_h2(m, [a]))
+            else:
+                result = leave_bank(sum_of_h2(m, [0, 1]), "result%d" % m, scale_on_vector)
+            pair = fetch_pairs(result, l_n6, l_n7, "last_pair%d" % m)
+            larger = pick(pair, ALU.max, "last_larger%d" % m)
+            put(result, l_n6, larger)
+            nc.sync.dma_start(out[m * P : (m + 1) * P, :], result[:])

from contextlib import ExitStack

import concourse.mybir as mybir
from concourse.masks import make_identity

K, T, S, G, H, W = 512, 1024, 256, 2048, 512, 128
FLOPS = 5 * 2 * K * H * S

F32 = mybir.dt.float32
BF16 = mybir.dt.bfloat16
U32 = mybir.dt.uint32
I32 = mybir.dt.int32
U16 = mybir.dt.uint16
U8 = mybir.dt.uint8
FP8X4 = mybir.dt.float8_e4m3fn_x4
ACT = mybir.ActivationFunctionType
ALU = mybir.AluOpType

P = 128
TILES = H // P
HALF = H // 2
GROUP = 16
QUAD = 32
BLOCK = 8
SCALE_ROWS = K // 32
ALIGN = 64
SIXTEENTH = 0.0625


def tile_picked_mthhzmteordfill_none_p_kernel(
    tc, x_words, x_scales, d_words, d_scales, sl, th, gs,
    offs, k1, hz, k2, hy, k3, n1, n2, n3, n4, n5, k4, k5, two, n6, n7, out,
):
    nc = tc.nc
    with ExitStack() as ctx:
        lists = ctx.enter_context(tc.tile_pool(name="lists", bufs=1))
        work = ctx.enter_context(tc.tile_pool(name="work", bufs=1))
        sum_banks = ctx.enter_context(tc.psum_pool(name="sums", bufs=TILES))
        turn_banks = ctx.enter_context(tc.psum_pool(name="turns", bufs=2))

        def tile(shape, dtype, name, over=None):
            return work.tile(shape, dtype, name=name, tag=over or name, align_bytes=ALIGN)

        def load_list(ap, name):
            offsets = lists.tile(list(ap.shape), U16, name=name)
            nc.sync.dma_start(offsets[:], ap)
            return offsets

        def entries(offsets, first, count):
            return offsets[:, first // GROUP : (first + count) // GROUP]

        def gather_parts(name, dtype, parts, over=None):
            picked = tile([P, sum(part[3] for part in parts)], dtype, name, over)
            at = 0
            for window, offsets, first, count in parts:
                nc.vector.tensor_copy(picked[:, at : at + count], window[:].indirect(entries(offsets, first, count)))
                at = at + count
            return picked

        def place_scales(plane, picked):
            for q in range(P // QUAD):
                nc.sync.dma_start(
                    plane[QUAD * q : QUAD * q + QUAD // BLOCK, :].bitcast(I32),
                    picked[QUAD * q : QUAD * (q + 1) : BLOCK, :].bitcast(I32),
                )

        x_byte_table = tile([P, T], U8, "x_byte_table")
        d_byte_table = tile([P, G], U8, "d_byte_table")
        x_word_table = tile([P, T], U32, "x_word_table")
        d_word_table = tile([P, G], U32, "d_word_table")
        plane_first = tile([P, 3 * S + 3 * HALF], U8, "plane_first")
        plane_second = tile([P, 3 * HALF], U8, "plane_second")
        plane_two_k4 = tile([P, S + H], U8, "plane_two_k4")
        plane_k5 = tile([P, H], U8, "plane_k5")
        z_planes = [tile([P, W], U8, "z_plane%d" % a) for a in range(2)]
        for zeroed in (d_byte_table, plane_first, plane_second, plane_two_k4, plane_k5):
            nc.vector.memset(zeroed[:].bitcast(I32), 0)

        x_rows = x_scales[0].bitcast(I32).unsqueeze(1).to_broadcast([SCALE_ROWS, BLOCK, T // 4])
        nc.scalar.dma_start(x_byte_table[:].bitcast(I32), x_rows)
        l_offs, l_hz, l_hy = load_list(offs, "offs"), load_list(hz, "hz"), load_list(hy, "hy")
        nc.sync.dma_start(d_byte_table[0:P:BLOCK, :].bitcast(I32), d_scales[0].bitcast(I32))
        l_k1, l_k2, l_k3 = load_list(k1, "k1"), load_list(k2, "k2"), load_list(k3, "k3")
        nc.sync.dma_start(x_word_table[:].bitcast(I32), x_words[0].rearrange("p n t -> p (n t)").bitcast(I32))
        l_n1, l_n2 = load_list(n1, "n1"), load_list(n2, "n2")
        l_n3, l_n4, l_n5 = load_list(n3, "n3"), load_list(n4, "n4"), load_list(n5, "n5")
        l_two = load_list(two, "two")
        nc.sync.dma_start(d_word_table[:].bitcast(I32), d_words[0].rearrange("p n t -> p (n t)").bitcast(I32))

        vectors = tile([P, P], F32, "vectors")
        nc.gpsimd.memset(vectors[:], 0.0)
        for v, vec in enumerate((sl, th, gs)):
            nc.gpsimd.dma_start(vectors[TILES * v : TILES * (v + 1), :], vec.rearrange("(t p) o -> t (p o)", p=P))
        ident_bf16 = tile([P, P], BF16, "ident_bf16")
        ident_f32 = tile([P, P], F32, "ident_f32")
        make_identity(nc, ident_bf16[:])
        make_identity(nc, ident_f32[:])
        warm = tile([P, 1], F32, "warm")
        nc.scalar.activation(warm[:], ident_f32[:, 0:1], ACT.Sigmoid)

        vector_bank = turn_banks.tile([P, P], F32, name="turn_one")
        nc.tensor.transpose(vector_bank[:], vectors[:], ident_f32[:])
        columns = tile([P, 3 * TILES], F32, "columns")
        nc.scalar.copy(columns[:], vector_bank[:, : 3 * TILES])
        slope, level, gain = (columns[:, TILES * v : TILES * (v + 1)] for v in range(3))

        x_lists, d_lists = (l_offs, l_hz, l_hy), (l_k1, l_k2, l_k3)
        bytes_first = gather_parts(
            "bytes_first", U8,
            [(x_byte_table, lst, 0, S) for lst in x_lists] + [(d_byte_table, lst, 0, HALF) for lst in d_lists],
        )
        place_scales(plane_first, bytes_first)

        l_k4, l_k5 = load_list(k4, "k4"), load_list(k5, "k5")
        l_n6, l_n7 = load_list(n6, "n6"), load_list(n7, "n7")
        slope_level = tile([P, TILES], F32, "slope_level")
        bias = tile([P, TILES], F32, "bias")
        nc.gpsimd.tensor_tensor(slope_level[:], slope, level, ALU.mult)
        nc.gpsimd.tensor_scalar(bias[:], slope_level[:], -1.0, 0.0, ALU.mult, ALU.add)

        x_picked = gather_parts("x_picked", U32, [(x_word_table, lst, 0, S) for lst in x_lists])
        words_first = gather_parts("words_first", U32, [(d_word_table, lst, 0, HALF) for lst in d_lists])

        def sum_of_h(t, words, plane):
            acc = sum_banks.tile([P, S], F32, name="acc")
            c = (t % 2) * P
            for n in range(3):
                nc.tensor.matmul_mx(
                    out=acc[:],
                    lhsT=words[n][:, c : c + P].bitcast(FP8X4),
                    lhsT_scale=plane[:, n * HALF + c : n * HALF + c + P],
                    rhs=x_picked[:, n * S : (n + 1) * S].bitcast(FP8X4),
                    rhs_scale=plane_first[:, n * S : (n + 1) * S],
                    start=(n == 0),
                    stop=(n == 2),
                )
            return acc

        def scale_on_scalar(dst, acc):
            nc.scalar.activation(dst, acc[:], ACT.Copy, scale=SIXTEENTH)

        def scale_on_vector(dst, acc):
            nc.vector.tensor_scalar(dst, acc[:], SIXTEENTH, None, ALU.mult)

        def leave_bank(acc, name, scale_out):
            result = tile([P, S], F32, name)
            scale_out(result[:], acc)
            return result

        def fetch_pairs(rows, list_a, list_b, name):
            pair = tile([P, 2 * W], F32, name)
            nc.scalar.activation(pair[:, :W], rows[:].indirect(list_a[:]), ACT.Copy)
            nc.scalar.activation(pair[:, W:], rows[:].indirect(list_b[:]), ACT.Copy)
            return pair

        def pick(pair, op, name, over=None):
            chosen = tile([P, W], F32, name, over)
            nc.vector.tensor_tensor(chosen[:], pair[:, :W], pair[:, W:], op)
            return chosen

        def put(window, offsets, values):
            nc.scalar.activation(window[:].indirect(offsets[:]), values[:], ACT.Copy)

        ub = [tile([P, S], F32, "ub%d" % t) for t in range(TILES)]
        sg = [tile([P, S], F32, "sg%d" % t) for t in range(TILES)]

        def put_both(tiles, larger, smaller):
            for offsets, values in ((l_n3, larger), (l_n4, smaller)):
                for t, chosen in zip(tiles, values):
                    put(ub[t], offsets, chosen)

        def gate(t, a):
            nc.scalar.activation(
                sg[t][:, a * W : (a + 1) * W],
                ub[t][:].indirect(entries(l_n5, a * W, W)),
                ACT.Sigmoid,
                scale=slope[:, t : t + 1],
                bias=bias[:, t : t + 1],
            )

        def weigh(t, first, count, name, over=None):
            z = tile([P, count], BF16, name, over)
            cols = slice(first, first + count)
            nc.vector.scalar_tensor_tensor(z[:], ub[t][:, cols], gain[:, t : t + 1], sg[t][:, cols], ALU.mult, ALU.mult)
            return z

        z_turned = tile([P, 2, 2, P], F32, "z_turned")

        first_parts = [words_first[:, n * HALF : (n + 1) * HALF] for n in range(3)]
        acc0 = sum_of_h(0, first_parts, plane_first[:, 3 * S :])
        acc1 = sum_of_h(1, first_parts, plane_first[:, 3 * S :])

        bytes_k12 = gather_parts(
            "bytes_k12", U8, [(d_byte_table, lst, HALF, HALF) for lst in (l_k1, l_k2)], over="bytes_first"
        )
        place_scales(plane_second[:, : 2 * HALF], bytes_k12)

        h0 = leave_bank(acc0, "h0", scale_on_scalar)
        pair0 = fetch_pairs(h0, l_n1, l_n2, "pair0")
        h1 = leave_bank(acc1, "h1", scale_on_vector)
        bytes_k3 = gather_parts("bytes_k3", U8, [(d_byte_table, l_k3, HALF, HALF)], over="words_first")
        place_scales(plane_second[:, 2 * HALF :], bytes_k3)
        pair1 = fetch_pairs(h1, l_n1, l_n2, "pair1")
        larger0 = pick(pair0, ALU.max, "larger0")
        words_k1 = gather_parts("words_k1", U32, [(d_word_table, l_k1, HALF, HALF)], over="h0")
        larger1 = pick(pair1, ALU.max, "larger1")
        smaller0 = pick(pair0, ALU.min, "smaller0", over="h1")
        smaller1 = pick(pair1, ALU.min, "smaller1")
        put_both((0, 1), (larger0, larger1), (smaller0, smaller1))
        for t in (0, 1):
            for a in range(2):
                gate(t, a)

        words_k23 = gather_parts(
            "words_k23", U32, [(d_word_table, lst, HALF, HALF) for lst in (l_k2, l_k3)], over="pair0"
        )
        words_two = gather_parts("words_two", U32, [(x_word_table, l_two, 0, S)], over="pair1")

        second_parts = [words_k1[:], words_k23[:, :HALF], words_k23[:, HALF:]]
        acc2 = sum_of_h(2, second_parts, plane_second)
        acc3 = sum_of_h(3, second_parts, plane_second)
        h2 = leave_bank(acc2, "h2", scale_on_vector)
        h3 = leave_bank(acc3, "h3", scale_on_vector)

        bytes_two_k4 = gather_parts(
            "bytes_two_k4", U8, [(x_byte_table, l_two, 0, S), (d_byte_table, l_k4, 0, H)], over="x_picked"
        )
        place_scales(plane_two_k4, bytes_two_k4)

        pair2 = fetch_pairs(h2, l_n1, l_n2, "pair2")
        pair3 = fetch_pairs(h3, l_n1, l_n2, "pair3")
        larger2 = pick(pair2, ALU.max, "larger2")
        z0 = weigh(0, 0, S, "z0", over="h2")
        larger3 = pick(pair3, ALU.max, "larger3")
        smaller2 = pick(pair2, ALU.min, "smaller2", over="h3")
        smaller3 = pick(pair3, ALU.min, "smaller3")
        z1 = weigh(1, 0, S, "z1", over="pair2")
        put_both((2, 3), (larger2, larger3), (smaller2, smaller3))
        for a in range(2):
            for t in (2, 3):
                gate(t, a)

        early_bank = turn_banks.tile([P, 2, 2, P], BF16, name="turn_one")
        for t, z in enumerate((z0, z1)):
            for a in range(2):
                nc.tensor.transpose(early_bank[:, a, t, :], z[:, a * W : (a + 1) * W], ident_bf16[:])
        nc.vector.tensor_copy(
            z_turned[:, :, :, : P // 2],
            early_bank[:].rearrange("j a t i -> j a (t i)").bitcast(F32).rearrange("j a (p u) -> j a u p", u=2),
        )

        bytes_k5 = gather_parts("bytes_k5", U8, [(d_byte_table, l_k5, 0, H)], over="pair3")
        place_scales(plane_k5, bytes_k5)
        words_low = gather_parts("words_low", U32, [(d_word_table, lst, 0, HALF) for lst in (l_k4, l_k5)], over="sg1")

        for a in range(2):
            late_bank = turn_banks.tile([P, 2, P], BF16, name="turn_one")
            for t in (2, 3):
                z = weigh(t, a * W, W, "z%d_%d" % (t, a))
                nc.tensor.transpose(late_bank[:, t - 2, :], z[:], ident_bf16[:])
            nc.scalar.copy(
                z_turned[:, a, :, P // 2 :],
                late_bank[:].rearrange("j t i -> j (t i)").bitcast(F32).rearrange("j (p u) -> j u p", u=2),
            )
        words_high = gather_parts(
            "words_high", U32, [(d_word_table, lst, HALF, HALF) for lst in (l_k4, l_k5)], over="sg3"
        )

        z_words = []
        for a in range(2):
            back_bank = turn_banks.tile([P, 2, P], F32, name="turn_two")
            for u in range(2):
                nc.tensor.transpose(back_bank[:, u, :], z_turned[:, a, u, :], ident_f32[:])
            z_rows = tile([P, W, 2], F32, "z_rows%d" % a)
            nc.scalar.copy(z_rows[:], back_bank[:].rearrange("p u j -> p j u"))
            codes = tile([P, W], U32, "z_words%d" % a)
            nc.vector.quantize_mx(
                out=codes[:].bitcast(FP8X4),
                scales=z_planes[a][:],
                in_=z_rows[:].rearrange("p j u -> p (j u)").bitcast(BF16),
            )
            z_words.append(codes)

        def sum_of_h2(m, halves):
            words = words_low if m < 2 else words_high
            c = (m % 2) * P
            cols = slice(halves[0] * W, (halves[-1] + 1) * W)
            if m < 2:
                acc = sum_banks.tile([P, len(halves) * W], F32, name="acc")
            else:
                acc = turn_banks.tile([P, len(halves) * W], F32, name="turn_two")
            nc.tensor.matmul_mx(
                out=acc[:],
                lhsT=words[:, HALF + c : HALF + c + P].bitcast(FP8X4),
                lhsT_scale=plane_k5[:, m * P : (m + 1) * P],
                rhs=words_two[:, cols].bitcast(FP8X4),
                rhs_scale=plane_two_k4[:, cols],
                start=True,
                stop=False,
            )
            for a in halves:
                nc.tensor.matmul_mx(
                    out=acc[:, (a - halves[0]) * W : (a - halves[0] + 1) * W],
                    lhsT=words[:, c : c + P].bitcast(FP8X4),
                    lhsT_scale=plane_two_k4[:, S + m * P : S + (m + 1) * P],
                    rhs=z_words[a][:].bitcast(FP8X4),
                    rhs_scale=z_planes[a][:],
                    start=False,
                    stop=(a == halves[-1]),
                )
            return acc

        for m in range(TILES):
            if m == 0:
                result = tile([P, S], F32, "result0")
                for a in range(2):
                    scale_on_scalar(result[:, a * W : (a + 1) * W], sum_of_h2(m, [a]))
            else:
                result = leave_bank(sum_of_h2(m, [0, 1]), "result%d" % m, scale_on_vector)
            pair = fetch_pairs(result, l_n6, l_n7, "last_pair%d" % m)
            larger = pick(pair, ALU.max, "last_larger%d" % m)
            put(result, l_n6, larger)
            nc.sync.dma_start(out[m * P : (m + 1) * P, :], result[:])
